import numpy as np
import ml_dtypes


def mxq(x, axis, fmt="e4m3"):
    dtype, down = {"e4m3": (ml_dtypes.float8_e4m3fn, 7), "e5m2": (ml_dtypes.float8_e5m2, 14)}[fmt]
    v = np.moveaxis(np.asarray(x, np.float32).astype(ml_dtypes.bfloat16).astype(np.float64), axis, -1)
    blocks = v.reshape(v.shape[:-1] + (-1, 32))
    amax = np.abs(blocks).max(-1, keepdims=True)
    byte = np.maximum(np.where(amax > 0, np.frexp(amax)[1] - 1 + 127, 0) - down, 1)
    scale = np.exp2(byte - 127.0)
    codes = (blocks / scale).astype(np.float32).astype(dtype).astype(np.float64)
    return np.moveaxis((codes * scale).reshape(v.shape), -1, axis)


WIDE = False


def mx_kscale(k):
    if not WIDE:
        return np.ones(k)
    levels = np.array([10, -10, 5, -5, 0])
    if k % 512:
        return np.exp2(np.random.permutation(np.resize(levels, k // 32))).repeat(32)
    a = np.empty((k // 512, 16))
    for p in range(k // 512):
        a[p, :8] = np.random.permutation(np.resize(levels, 8))
        for g in range(8):
            far = levels[np.abs(levels - a[p, g]) >= 10]
            a[p, g + 8] = far[np.random.randint(len(far))]
    return np.exp2(a.ravel()).repeat(32)


BF16 = ml_dtypes.bfloat16


def bf(x):
    return np.asarray(x, np.float32).astype(BF16)


def f64(x):
    return np.asarray(x).astype(np.float64)


B, H, S, M, E = 16, 2, 512, 512, 128


def joint_exp(lc, lm):
    mx = np.maximum(np.max(lc, axis=-1, keepdims=True), np.max(lm, axis=-1, keepdims=True))
    ec = np.exp(lc - mx)
    em = np.exp(lm - mx)
    z = np.sum(ec, axis=-1, keepdims=True) + np.sum(em, axis=-1, keepdims=True)
    return ec, em, z


def draw0():
    s, t = mx_kscale(S), mx_kscale(M)
    kscale = 1.0 / np.sqrt(E)
    return {
        "q": bf(np.random.standard_normal((B, H, S, E)) * 2.0),
        "k": bf(np.random.standard_normal((B, H, S, E)) * kscale),
        "v": bf(np.random.standard_normal((B, H, S, E)) * s[:, None]),
        "km": bf(np.random.standard_normal((H, M, E)) * kscale),
        "vm": bf(np.random.standard_normal((H, M, E)) * t[:, None]),
        "tg": bf(np.random.standard_normal((H, S)) / s),
        "mg": bf(np.random.standard_normal((H, M)) / t),
    }


def core(q, k, v, km, vm, tg, mg):
    lc = f64(q) @ f64(k).transpose(0, 1, 3, 2)
    lm = f64(q) @ f64(km).transpose(0, 2, 1)
    ec, em, z = joint_exp(lc, lm)
    pc = ec / z * f64(tg)[None, :, None, :]
    pm = em / z * f64(mg)[None, :, None, :]
    yc = mxq(pc, 3, "e4m3") @ mxq(f64(v), 2, "e4m3")
    ym = mxq(pm, 3, "e4m3") @ mxq(f64(vm), 1, "e4m3")
    return yc + ym


def e4m3fn_bytes(y):
    return np.clip(np.asarray(y, np.float64), -448.0, 448.0).astype(np.float32).astype(ml_dtypes.float8_e4m3fn).view(np.uint8)


def e4m3fn_values(b):
    return np.asarray(b, np.uint8).view(ml_dtypes.float8_e4m3fn).astype(np.float64)


def setup_inputs():
    d = draw0()
    x0 = np.asarray(d['v']).astype(np.float64)
    s = (np.max(np.abs(x0), axis=(0, 1, 3), keepdims=True) / 448.0).astype(np.float32)
    out = {}
    for k, v in d.items():
        if k == 'v':
            out['v_bytes'] = e4m3fn_bytes(x0 / s.astype(np.float64))
            out['v_scale'] = s
        else:
            out[k] = v
    return out


def reference(q, k, v_bytes, v_scale, km, vm, tg, mg):
    return core(q, k, e4m3fn_values(v_bytes) * v_scale.astype(np.float64), km, vm, tg, mg)

@@ -1,0 +1,338 @@
+from contextlib import ExitStack
+
+import concourse.mybir as mybir
+from concourse.masks import make_identity
+
+B, H, S, E = 16, 2, 512, 128
+FLOPS = 2 * 2 * B * H * S * (2 * S) * E
+
+F32 = mybir.dt.float32
+BF16 = mybir.dt.bfloat16
+U32 = mybir.dt.uint32
+U8 = mybir.dt.uint8
+FP8 = mybir.dt.float8_e4m3fn
+FP8X4 = mybir.dt.float8_e4m3fn_x4
+ALU = mybir.AluOpType
+ACT = mybir.ActivationFunctionType
+
+P = 128
+PACK = 4
+KEYS = 2 * S
+GROUPS = B * H
+TILES = S // P
+POOL_COLS = 768
+
+
+def tile_allattentionpersistentmemoryheads_t_kernel(tc, q, k, v_bytes, v_scale, km, vm, tg, mg, out):
+    nc = tc.nc
+
+    with ExitStack() as ctx:
+        keep = ctx.enter_context(tc.tile_pool(name="keep", bufs=1))
+        work = ctx.enter_context(tc.tile_pool(name="work", bufs=3))
+        psum = ctx.enter_context(tc.psum_pool(name="psum", bufs=1))
+        ctx.enter_context(tc.manual_schedule())
+
+        q_rows, k_rows, v_raw, qk_t, v_wide, v_inter = {}, {}, {}, {}, {}, {}
+        banks, neg_logits, neg_max, sums, recips, exps, probs = {}, {}, {}, {}, {}, {}, {}
+        turned, probs_t, p_codes, p_scales, v_codes, v_scales, gate_bank = {}, {}, {}, {}, {}, {}, {}
+        bank_count = []
+
+        def live(g):
+            return 0 <= g < GROUPS
+
+        def head(g):
+            return g // B
+
+        def batch(g):
+            return g % B
+
+        def load_qk(g):
+            if live(g):
+                q_rows[g] = work.tile([P, PACK, E], BF16, name="q_rows")
+                k_rows[g] = work.tile([P, PACK, E], BF16, name="k_rows")
+                nc.sync.dma_start(out=q_rows[g][:], in_=q[batch(g), head(g)].rearrange("(p t) e -> p t e", t=PACK))
+                nc.sync.dma_start(out=k_rows[g][:], in_=k[batch(g), head(g)].rearrange("(p t) e -> p t e", t=PACK))
+
+        def load_v(g):
+            if live(g):
+                v_raw[g] = work.tile([P, PACK * E], U8, name="v_raw", align_bytes=64)
+                nc.sync.dma_start(
+                    out=v_raw[g][:], in_=v_bytes[batch(g), head(g)].rearrange("(p t) e -> p (t e)", t=PACK)
+                )
+
+        def turn_rows(first, second):
+            bank = psum.tile([P, 2 * PACK, P], BF16, name="rows_bank")
+            for n, rows in enumerate((first, second)):
+                for t in range(PACK):
+                    nc.tensor.transpose(bank[:, n * PACK + t, :], rows[:, t, :], ident_bf16[:])
+            return bank
+
+        def turn_qk(g):
+            if live(g):
+                turned["qk", g] = turn_rows(q_rows[g], k_rows[g])
+
+        def copy_qk(g):
+            if live(g):
+                qk_t[g] = work.tile([P, 2 * PACK, P], BF16, name="qk_t")
+                nc.scalar.copy(out=qk_t[g][:], in_=turned["qk", g][:])
+
+        def logits(g, i, half):
+            if live(g):
+                bank = psum.tile([P, S], F32, name="logit_bank%d" % (len(bank_count) % 3))
+                bank_count.append(1)
+                banks[g, i, half] = bank
+                if half == 0:
+                    keys = qk_t[g][:, PACK:, :]
+                else:
+                    keys = km_t[:, head(g) * PACK : (head(g) + 1) * PACK, :]
+                nc.tensor.matmul(
+                    out=bank[:], lhsT=qk_t[g][:, i, :], rhs=keys.rearrange("e t p -> e (t p)"), start=True, stop=True
+                )
+
+        def scan_logits(g, i, half):
+            if live(g):
+                if half == 0:
+                    neg_logits[g, i] = work.tile([P, KEYS], F32, name="neg_logits", bufs=4)
+                    if i == 0:
+                        neg_max[g] = work.tile([P, TILES, 2], F32, name="neg_max")
+                nc.vector.tensor_scalar(
+                    out=neg_logits[g, i][:, half * S : (half + 1) * S].rearrange("q (u p e) -> q u p e", u=2, e=2),
+                    in0=banks[g, i, half][:].rearrange("q (u e p) -> q u p e", u=2, e=2),
+                    scalar1=-1.0,
+                    scalar2=None if half == 0 else neg_max[g][:, i, 0:1],
+                    op0=ALU.mult,
+                    op1=ALU.min,
+                    accum_out=neg_max[g][:, i, half : half + 1],
+                )
+
+        def exponentials(g, i):
+            if live(g):
+                if i == 0:
+                    sums[g] = work.tile([P, TILES], F32, name="sums")
+                if i % 2 == 0:
+                    exps[g, i // 2] = work.tile([P, 2, KEYS], F32, name="exps", bufs=5)
+                nc.scalar.activation(
+                    out=exps[g, i // 2][:, i % 2, :],
+                    in_=neg_logits[g, i][:],
+                    func=ACT.Exp,
+                    bias=neg_max[g][:, i, 1:2],
+                    scale=-1.0,
+                    accum_out=sums[g][:, i : i + 1],
+                )
+
+        def reciprocals(g):
+            if live(g):
+                recips[g] = work.tile([P, TILES], F32, name="recips")
+                nc.vector.reciprocal(out=recips[g][:], in_=sums[g][:])
+                for pair in range(2):
+                    probs[g, pair] = work.tile([P, 2, KEYS], BF16, name="probs", bufs=5, align_bytes=64)
+
+        def spread_gates(g):
+            if live(g) and batch(g) == 0:
+                bank = psum.tile([P, KEYS], BF16, name="gate_bank")
+                gate_bank[head(g)] = bank
+                for half in range(2):
+                    cols = slice(half * S, (half + 1) * S)
+                    nc.tensor.matmul(
+                        out=bank[:, cols], lhsT=ident_bf16[:], rhs=gates[:, head(g), cols], start=True, stop=True
+                    )
+
+        def weigh_on_pool(g):
+            if live(g):
+                pair = exps[g, 0]
+                for i in range(2):
+                    nc.gpsimd.tensor_scalar(
+                        out=pair[:, i, :POOL_COLS],
+                        in0=pair[:, i, :POOL_COLS],
+                        scalar1=recips[g][:, i : i + 1],
+                        scalar2=0.0,
+                        op0=ALU.mult,
+                        op1=ALU.add,
+                    )
+                nc.gpsimd.tensor_tensor(
+                    out=probs[g, 0][:, :, :POOL_COLS],
+                    in0=pair[:, :, :POOL_COLS],
+                    in1=gates[:, head(g), :POOL_COLS].unsqueeze(1).to_broadcast([P, 2, POOL_COLS]),
+                    op=ALU.mult,
+                )
+
+        def weigh_on_vector(g, i):
+            if live(g):
+                cols = slice(POOL_COLS if i < 2 else 0, KEYS)
+                nc.vector.scalar_tensor_tensor(
+                    out=probs[g, i // 2][:, i % 2, cols],
+                    in0=exps[g, i // 2][:, i % 2, cols],
+                    scalar=recips[g][:, i : i + 1],
+                    in1=gate_bank[head(g)][:, cols],
+                    op0=ALU.mult,
+                    op1=ALU.mult,
+                )
+
+        def turn_probs(g, i):
+            if live(g):
+                bank = psum.tile([P, PACK, P], F32, name="probs_bank%d" % (i % 2))
+                turned["p", g, i] = bank
+                words = probs[g, i // 2][:, i % 2, :].bitcast(F32)
+                for n in range(PACK):
+                    nc.tensor.transpose(bank[:, n, :], words[:, n * P : (n + 1) * P], ident_f32[:])
+
+        def copy_probs(g, i):
+            if live(g):
+                if i == 0:
+                    probs_t[g] = work.tile([P, TILES * KEYS], BF16, name="probs_t", align_bytes=64)
+                nc.scalar.copy(
+                    out=probs_t[g][:, i * KEYS : (i + 1) * KEYS].bitcast(F32).rearrange("p (c q u) -> p c q u", c=2, u=2),
+                    in_=turned["p", g, i][:].rearrange("p (c u) q -> p c q u", u=2),
+                )
+
+        def widen_v(g):
+            if live(g):
+                v_wide[g] = work.tile([P, PACK, E], BF16, name="v_wide")
+                for t in range(PACK):
+                    nc.scalar.activation(
+                        out=v_wide[g][:, t, :],
+                        in_=v_raw[g][:, t * E : (t + 1) * E].bitcast(FP8),
+                        func=ACT.Copy,
+                        scale=scale_cols[:, t : t + 1],
+                    )
+
+        def interleave_v(g):
+            if live(g):
+                v_inter[g] = work.tile([P, E, PACK], BF16, name="v_inter", align_bytes=64)
+                nc.scalar.copy(out=v_inter[g][:], in_=v_wide[g][:].rearrange("p t e -> p e t"))
+
+        def quantize(g):
+            if live(g):
+                p_codes[g] = work.tile([P, TILES * 2 * P], U32, name="p_codes", align_bytes=64)
+                p_scales[g] = work.tile([P, TILES * 2 * P], U8, name="p_scales", align_bytes=64)
+                v_codes[g] = work.tile([P, E], U32, name="v_codes", align_bytes=64)
+                v_scales[g] = work.tile([P, E], U8, name="v_scales", align_bytes=64)
+                nc.vector.quantize_mx(out=p_codes[g][:].bitcast(FP8X4), scales=p_scales[g][:], in_=probs_t[g][:])
+                nc.vector.quantize_mx(
+                    out=v_codes[g][:].bitcast(FP8X4),
+                    scales=v_scales[g][:],
+                    in_=v_inter[g][:].rearrange("p e t -> p (e t)"),
+                )
+
+        def mix_values(g):
+            if live(g):
+                bank = psum.tile([P, TILES, E], F32, name="out_bank")
+                mem = slice(head(g) * E, (head(g) + 1) * E)
+                for i in range(TILES):
+                    for half in range(2):
+                        cols = slice((2 * i + half) * P, (2 * i + half + 1) * P)
+                        nc.tensor.matmul_mx(
+                            out=bank[:, i, :],
+                            lhsT=p_codes[g][:, cols].bitcast(FP8X4),
+                            lhsT_scale=p_scales[g][:, cols],
+                            rhs=(v_codes[g][:] if half == 0 else vm_codes[:, mem]).bitcast(FP8X4),
+                            rhs_scale=v_scales[g][:] if half == 0 else vm_scales[:, mem],
+                            start=(half == 0),
+                            stop=(half == 1),
+                        )
+                result = work.tile([P, TILES, E], F32, name="result")
+                nc.scalar.copy(out=result[:], in_=bank[:])
+                nc.sync.dma_start(out=out[batch(g), head(g)].rearrange("(p t) e -> p t e", t=PACK), in_=result[:])
+
+        load_qk(0)
+        km_rows = keep.tile([P, H, PACK, E], BF16)
+        nc.sync.dma_start(
+            out=km_rows[:].rearrange("p h t e -> p h (t e)"), in_=km.rearrange("h (p t) e -> p h (t e)", t=PACK)
+        )
+        load_qk(1)
+        gate_rows = []
+        for name, row in (("tg_rows", tg), ("mg_rows", mg)):
+            rows = keep.tile([P, H * S], BF16, name=name)
+            nc.sync.dma_start(out=rows[:], in_=row.rearrange("h s -> (h s)").partition_broadcast(P))
+            gate_rows.append(rows)
+        vm_rows = keep.tile([P, H, PACK, E], BF16)
+        nc.sync.dma_start(
+            out=vm_rows[:].rearrange("p h t e -> p h (t e)"), in_=vm.rearrange("h (p t) e -> p h (t e)", t=PACK)
+        )
+        scale_cols = keep.tile([P, PACK], F32)
+        nc.sync.dma_start(out=scale_cols[:], in_=v_scale.rearrange("a b (p t) c -> p (a b t c)", t=PACK))
+
+        warm = keep.tile([P, 1], F32)
+        nc.vector.memset(warm[:], 0.0)
+        nc.scalar.activation(out=warm[:], in_=warm[:], func=ACT.Exp)
+
+        ident_bf16 = keep.tile([P, P], BF16)
+        make_identity(nc, ident_bf16[:])
+        ident_f32 = keep.tile([P, P], F32)
+        make_identity(nc, ident_f32[:])
+
+        turn_qk(0)
+        copy_qk(0)
+        km_bank = turn_rows(km_rows[:, 0], km_rows[:, 1])
+        km_t = keep.tile([P, H * PACK, P], BF16)
+        nc.scalar.copy(out=km_t[:], in_=km_bank[:])
+
+        gates = keep.tile([P, H, KEYS], BF16)
+        for h in range(H):
+            for half in range(2):
+                nc.gpsimd.tensor_copy(
+                    out=gates[:, h, half * S : (half + 1) * S].rearrange("x (u p e) -> x u p e", u=2, e=2),
+                    in_=gate_rows[half][:, h * S : (h + 1) * S].rearrange("x (p u e) -> x u p e", u=2, e=2),
+                )
+        vm_inter = keep.tile([P, H, E, PACK], BF16, align_bytes=64)
+        vm_codes = keep.tile([P, H * E], U32, align_bytes=64)
+        vm_scales = keep.tile([P, H * E], U8, align_bytes=64)
+
+        logits(0, 0, 0)
+        logits(0, 1, 0)
+        logits(0, 0, 1)
+
+        for g in range(GROUPS + 3):
+            load_qk(g + 2)
+            load_v(g - 1)
+            quantize(g - 3)
+            if g == 1:
+                nc.vector.quantize_mx(
+                    out=vm_codes[:].bitcast(FP8X4),
+                    scales=vm_scales[:],
+                    in_=vm_inter[:].rearrange("p h e t -> p (h e t)"),
+                )
+            reciprocals(g - 1)
+            weigh_on_pool(g - 1)
+            spread_gates(g - 1)
+            turn_probs(g - 2, 0)
+            turn_probs(g - 2, 1)
+            copy_probs(g - 2, 0)
+            turn_probs(g - 2, 2)
+            copy_probs(g - 2, 1)
+            turn_probs(g - 2, 3)
+            copy_probs(g - 2, 2)
+            copy_probs(g - 2, 3)
+            mix_values(g - 3)
+
+            scan_logits(g, 0, 0)
+            logits(g, 2, 0)
+            scan_logits(g, 1, 0)
+            logits(g, 1, 1)
+            scan_logits(g, 0, 1)
+            exponentials(g, 0)
+            turn_qk(g + 1)
+            weigh_on_vector(g - 1, 0)
+            logits(g, 3, 0)
+            copy_qk(g + 1)
+            scan_logits(g, 2, 0)
+            logits(g, 2, 1)
+            scan_logits(g, 1, 1)
+            exponentials(g, 1)
+            logits(g, 3, 1)
+            weigh_on_vector(g - 1, 1)
+            widen_v(g - 2)
+            if g == 0:
+                for h in range(H):
+                    nc.scalar.copy(out=vm_inter[:, h], in_=vm_rows[:, h].rearrange("p t e -> p e t"))
+            scan_logits(g, 3, 0)
+            logits(g + 1, 0, 0)
+            scan_logits(g, 2, 1)
+            exponentials(g, 2)
+            logits(g + 1, 1, 0)
+            weigh_on_vector(g - 1, 2)
+            interleave_v(g - 2)
+            scan_logits(g, 3, 1)
+            logits(g + 1, 0, 1)
+            exponentials(g, 3)
+            weigh_on_vector(g - 1, 3)

@@ -20,7 +20,7 @@ PACK = 4
 KEYS = 2 * S
 GROUPS = B * H
 TILES = S // P
-POOL_COLS = 768
+V_BATCH = 4
 
 
 def tile_allattentionpersistentmemoryheads_t_kernel(tc, q, k, v_bytes, v_scale, km, vm, tg, mg, out):
@@ -55,9 +55,11 @@ def tile_allattentionpersistentmemoryheads_t_kernel(tc, q, k, v_bytes, v_scale, 
 
         def load_v(g):
             if live(g):
-                v_raw[g] = work.tile([P, PACK * E], U8, name="v_raw", align_bytes=64)
+                n, b = divmod(g, V_BATCH)
+                if b == 0:
+                    v_raw[n] = work.tile([P, PACK, V_BATCH, E], U8, name="v_raw", align_bytes=64)
                 nc.sync.dma_start(
-                    out=v_raw[g][:], in_=v_bytes[batch(g), head(g)].rearrange("(p t) e -> p (t e)", t=PACK)
+                    out=v_raw[n][:, :, b, :], in_=v_bytes[batch(g), head(g)].rearrange("(p t) e -> p t e", t=PACK)
                 )
 
         def turn_rows(first, second):
@@ -92,7 +94,7 @@ def tile_allattentionpersistentmemoryheads_t_kernel(tc, q, k, v_bytes, v_scale, 
         def scan_logits(g, i, half):
             if live(g):
                 if half == 0:
-                    neg_logits[g, i] = work.tile([P, KEYS], F32, name="neg_logits", bufs=4)
+                    neg_logits[g, i] = work.tile([P, KEYS], F32, name="neg_logits", bufs=5)
                     if i == 0:
                         neg_max[g] = work.tile([P, TILES, 2], F32, name="neg_max")
                 nc.vector.tensor_scalar(
@@ -137,33 +139,35 @@ def tile_allattentionpersistentmemoryheads_t_kernel(tc, q, k, v_bytes, v_scale, 
                         out=bank[:, cols], lhsT=ident_bf16[:], rhs=gates[:, head(g), cols], start=True, stop=True
                     )
 
+        def pool_tiles(g):
+            return 1 if g == GROUPS - 1 else 2
+
         def weigh_on_pool(g):
             if live(g):
-                pair = exps[g, 0]
-                for i in range(2):
+                pair, n = exps[g, 0], pool_tiles(g)
+                for i in range(n):
                     nc.gpsimd.tensor_scalar(
-                        out=pair[:, i, :POOL_COLS],
-                        in0=pair[:, i, :POOL_COLS],
+                        out=pair[:, i, :],
+                        in0=pair[:, i, :],
                         scalar1=recips[g][:, i : i + 1],
                         scalar2=0.0,
                         op0=ALU.mult,
                         op1=ALU.add,
                     )
                 nc.gpsimd.tensor_tensor(
-                    out=probs[g, 0][:, :, :POOL_COLS],
-                    in0=pair[:, :, :POOL_COLS],
-                    in1=gates[:, head(g), :POOL_COLS].unsqueeze(1).to_broadcast([P, 2, POOL_COLS]),
+                    out=probs[g, 0][:, :n, :],
+                    in0=pair[:, :n, :],
+                    in1=gates[:, head(g), :].unsqueeze(1).to_broadcast([P, n, KEYS]),
                     op=ALU.mult,
                 )
 
         def weigh_on_vector(g, i):
-            if live(g):
-                cols = slice(POOL_COLS if i < 2 else 0, KEYS)
+            if live(g) and i >= pool_tiles(g):
                 nc.vector.scalar_tensor_tensor(
-                    out=probs[g, i // 2][:, i % 2, cols],
-                    in0=exps[g, i // 2][:, i % 2, cols],
+                    out=probs[g, i // 2][:, i % 2, :],
+                    in0=exps[g, i // 2][:, i % 2, :],
                     scalar=recips[g][:, i : i + 1],
-                    in1=gate_bank[head(g)][:, cols],
+                    in1=gate_bank[head(g)][:],
                     op0=ALU.mult,
                     op1=ALU.mult,
                 )
@@ -178,28 +182,42 @@ def tile_allattentionpersistentmemoryheads_t_kernel(tc, q, k, v_bytes, v_scale, 
 
         def copy_probs(g, i):
             if live(g):
-                if i == 0:
+                if i == 2:
                     probs_t[g] = work.tile([P, TILES * KEYS], BF16, name="probs_t", align_bytes=64)
                 nc.scalar.copy(
                     out=probs_t[g][:, i * KEYS : (i + 1) * KEYS].bitcast(F32).rearrange("p (c q u) -> p c q u", c=2, u=2),
                     in_=turned["p", g, i][:].rearrange("p (c u) q -> p c q u", u=2),
                 )
 
-        def widen_v(g):
-            if live(g):
-                v_wide[g] = work.tile([P, PACK, E], BF16, name="v_wide")
-                for t in range(PACK):
-                    nc.scalar.activation(
-                        out=v_wide[g][:, t, :],
-                        in_=v_raw[g][:, t * E : (t + 1) * E].bitcast(FP8),
-                        func=ACT.Copy,
-                        scale=scale_cols[:, t : t + 1],
-                    )
+        def widen_v(step):
+            n, t = divmod(step, PACK)
+            if live(n * V_BATCH):
+                if t == 0:
+                    v_wide[n] = work.tile([P, PACK, V_BATCH, E], BF16, name="v_wide")
+                nc.scalar.activation(
+                    out=v_wide[n][:, t].rearrange("p b e -> p (b e)"),
+                    in_=v_raw[n][:, t].rearrange("p b e -> p (b e)").bitcast(FP8),
+                    func=ACT.Copy,
+                    scale=scale_cols[:, t : t + 1],
+                )
 
         def interleave_v(g):
             if live(g):
+                n, b = divmod(g, V_BATCH)
+                bank = psum.tile([P, E, PACK], BF16, name="out_bank")
+                turned["v", g] = bank
+                nc.tensor.matmul(
+                    out=bank[:],
+                    lhsT=ident_bf16[:],
+                    rhs=v_wide[n][:, :, b, :].rearrange("p t e -> p e t"),
+                    start=True,
+                    stop=True,
+                )
+
+        def copy_v(g):
+            if live(g):
                 v_inter[g] = work.tile([P, E, PACK], BF16, name="v_inter", align_bytes=64)
-                nc.scalar.copy(out=v_inter[g][:], in_=v_wide[g][:].rearrange("p t e -> p e t"))
+                nc.scalar.copy(out=v_inter[g][:], in_=turned["v", g][:])
 
         def quantize(g):
             if live(g):
@@ -230,8 +248,12 @@ def tile_allattentionpersistentmemoryheads_t_kernel(tc, q, k, v_bytes, v_scale, 
                             start=(half == 0),
                             stop=(half == 1),
                         )
+                turned["out", g] = bank
+
+        def store(g):
+            if live(g):
                 result = work.tile([P, TILES, E], F32, name="result")
-                nc.scalar.copy(out=result[:], in_=bank[:])
+                nc.scalar.copy(out=result[:], in_=turned["out", g][:])
                 nc.sync.dma_start(out=out[batch(g), head(g)].rearrange("(p t) e -> p t e", t=PACK), in_=result[:])
 
         load_qk(0)
@@ -251,6 +273,8 @@ def tile_allattentionpersistentmemoryheads_t_kernel(tc, q, k, v_bytes, v_scale, 
         )
         scale_cols = keep.tile([P, PACK], F32)
         nc.sync.dma_start(out=scale_cols[:], in_=v_scale.rearrange("a b (p t) c -> p (a b t c)", t=PACK))
+        for g in range(7):
+            load_v(g)
 
         warm = keep.tile([P, 1], F32)
         nc.vector.memset(warm[:], 0.0)
@@ -284,7 +308,7 @@ def tile_allattentionpersistentmemoryheads_t_kernel(tc, q, k, v_bytes, v_scale, 
 
         for g in range(GROUPS + 3):
             load_qk(g + 2)
-            load_v(g - 1)
+            load_v(g + 7)
             quantize(g - 3)
             if g == 1:
                 nc.vector.quantize_mx(
@@ -295,15 +319,17 @@ def tile_allattentionpersistentmemoryheads_t_kernel(tc, q, k, v_bytes, v_scale, 
             reciprocals(g - 1)
             weigh_on_pool(g - 1)
             spread_gates(g - 1)
-            turn_probs(g - 2, 0)
-            turn_probs(g - 2, 1)
-            copy_probs(g - 2, 0)
-            turn_probs(g - 2, 2)
-            copy_probs(g - 2, 1)
             turn_probs(g - 2, 3)
+            turn_qk(g + 1)
             copy_probs(g - 2, 2)
+            copy_qk(g + 1)
+            turn_probs(g - 2, 0)
             copy_probs(g - 2, 3)
             mix_values(g - 3)
+            turn_probs(g - 2, 1)
+            copy_probs(g - 2, 0)
+            store(g - 3)
+            copy_probs(g - 2, 1)
 
             scan_logits(g, 0, 0)
             logits(g, 2, 0)
@@ -311,27 +337,28 @@ def tile_allattentionpersistentmemoryheads_t_kernel(tc, q, k, v_bytes, v_scale, 
             logits(g, 1, 1)
             scan_logits(g, 0, 1)
             exponentials(g, 0)
-            turn_qk(g + 1)
-            weigh_on_vector(g - 1, 0)
             logits(g, 3, 0)
-            copy_qk(g + 1)
             scan_logits(g, 2, 0)
             logits(g, 2, 1)
             scan_logits(g, 1, 1)
-            exponentials(g, 1)
             logits(g, 3, 1)
-            weigh_on_vector(g - 1, 1)
-            widen_v(g - 2)
+            interleave_v(g - 2)
             if g == 0:
                 for h in range(H):
                     nc.scalar.copy(out=vm_inter[:, h], in_=vm_rows[:, h].rearrange("p t e -> p e t"))
+                widen_v(0)
+                widen_v(1)
+            widen_v(g + 2)
+            exponentials(g, 1)
             scan_logits(g, 3, 0)
             logits(g + 1, 0, 0)
             scan_logits(g, 2, 1)
             exponentials(g, 2)
             logits(g + 1, 1, 0)
+            weigh_on_vector(g - 1, 1)
             weigh_on_vector(g - 1, 2)
-            interleave_v(g - 2)
+            turn_probs(g - 1, 2)
+            copy_v(g - 2)
             scan_logits(g, 3, 1)
             logits(g + 1, 0, 1)
             exponentials(g, 3)

@@ -21,6 +21,8 @@ KEYS = 2 * S
 GROUPS = B * H
 TILES = S // P
 V_BATCH = 4
+POOL_COLS = 896
+POOL_COLS_LAST = 384
 
 
 def tile_allattentionpersistentmemoryheads_t_kernel(tc, q, k, v_bytes, v_scale, km, vm, tg, mg, out):
@@ -62,16 +64,18 @@ def tile_allattentionpersistentmemoryheads_t_kernel(tc, q, k, v_bytes, v_scale, 
                     out=v_raw[n][:, :, b, :], in_=v_bytes[batch(g), head(g)].rearrange("(p t) e -> p t e", t=PACK)
                 )
 
-        def turn_rows(first, second):
-            bank = psum.tile([P, 2 * PACK, P], BF16, name="rows_bank")
-            for n, rows in enumerate((first, second)):
-                for t in range(PACK):
-                    nc.tensor.transpose(bank[:, n * PACK + t, :], rows[:, t, :], ident_bf16[:])
-            return bank
+        def turn_rows(bank, n, rows):
+            for t in range(PACK):
+                nc.tensor.transpose(bank[:, n * PACK + t, :], rows[:, t, :], ident_bf16[:])
 
-        def turn_qk(g):
+        def turn_q(g):
             if live(g):
-                turned["qk", g] = turn_rows(q_rows[g], k_rows[g])
+                turned["qk", g] = psum.tile([P, 2 * PACK, P], BF16, name="rows_bank")
+                turn_rows(turned["qk", g], 0, q_rows[g])
+
+        def turn_k(g):
+            if live(g):
+                turn_rows(turned["qk", g], 1, k_rows[g])
 
         def copy_qk(g):
             if live(g):
@@ -109,9 +113,8 @@ def tile_allattentionpersistentmemoryheads_t_kernel(tc, q, k, v_bytes, v_scale, 
 
         def exponentials(g, i):
             if live(g):
-                if i == 0:
-                    sums[g] = work.tile([P, TILES], F32, name="sums")
                 if i % 2 == 0:
+                    sums[g, i // 2] = work.tile([P, 2], F32, name="sums", bufs=4)
                     exps[g, i // 2] = work.tile([P, 2, KEYS], F32, name="exps", bufs=5)
                 nc.scalar.activation(
                     out=exps[g, i // 2][:, i % 2, :],
@@ -119,15 +122,14 @@ def tile_allattentionpersistentmemoryheads_t_kernel(tc, q, k, v_bytes, v_scale, 
                     func=ACT.Exp,
                     bias=neg_max[g][:, i, 1:2],
                     scale=-1.0,
-                    accum_out=sums[g][:, i : i + 1],
+                    accum_out=sums[g, i // 2][:, i % 2 : i % 2 + 1],
                 )
 
-        def reciprocals(g):
+        def reciprocals(g, pair):
             if live(g):
-                recips[g] = work.tile([P, TILES], F32, name="recips")
-                nc.vector.reciprocal(out=recips[g][:], in_=sums[g][:])
-                for pair in range(2):
-                    probs[g, pair] = work.tile([P, 2, KEYS], BF16, name="probs", bufs=5, align_bytes=64)
+                recips[g, pair] = work.tile([P, 2], F32, name="recips", bufs=4)
+                nc.vector.reciprocal(out=recips[g, pair][:], in_=sums[g, pair][:])
+                probs[g, pair] = work.tile([P, 2, KEYS], BF16, name="probs", bufs=5, align_bytes=64)
 
         def spread_gates(g):
             if live(g) and batch(g) == 0:
@@ -139,35 +141,36 @@ def tile_allattentionpersistentmemoryheads_t_kernel(tc, q, k, v_bytes, v_scale, 
                         out=bank[:, cols], lhsT=ident_bf16[:], rhs=gates[:, head(g), cols], start=True, stop=True
                     )
 
-        def pool_tiles(g):
-            return 1 if g == GROUPS - 1 else 2
+        def pool_cols(g):
+            return POOL_COLS_LAST if g == GROUPS - 1 else POOL_COLS
 
         def weigh_on_pool(g):
             if live(g):
-                pair, n = exps[g, 0], pool_tiles(g)
-                for i in range(n):
+                pair, n = exps[g, 0], pool_cols(g)
+                for i in range(2):
                     nc.gpsimd.tensor_scalar(
-                        out=pair[:, i, :],
-                        in0=pair[:, i, :],
-                        scalar1=recips[g][:, i : i + 1],
+                        out=pair[:, i, :n],
+                        in0=pair[:, i, :n],
+                        scalar1=recips[g, 0][:, i : i + 1],
                         scalar2=0.0,
                         op0=ALU.mult,
                         op1=ALU.add,
                     )
                 nc.gpsimd.tensor_tensor(
-                    out=probs[g, 0][:, :n, :],
-                    in0=pair[:, :n, :],
-                    in1=gates[:, head(g), :].unsqueeze(1).to_broadcast([P, n, KEYS]),
+                    out=probs[g, 0][:, :, :n],
+                    in0=pair[:, :, :n],
+                    in1=gates[:, head(g), :n].unsqueeze(1).to_broadcast([P, 2, n]),
                     op=ALU.mult,
                 )
 
         def weigh_on_vector(g, i):
-            if live(g) and i >= pool_tiles(g):
+            if live(g):
+                cols = slice(pool_cols(g) if i < 2 else 0, KEYS)
                 nc.vector.scalar_tensor_tensor(
-                    out=probs[g, i // 2][:, i % 2, :],
-                    in0=exps[g, i // 2][:, i % 2, :],
-                    scalar=recips[g][:, i : i + 1],
-                    in1=gate_bank[head(g)][:],
+                    out=probs[g, i // 2][:, i % 2, cols],
+                    in0=exps[g, i // 2][:, i % 2, cols],
+                    scalar=recips[g, i // 2][:, i % 2 : i % 2 + 1],
+                    in1=gate_bank[head(g)][:, cols],
                     op0=ALU.mult,
                     op1=ALU.mult,
                 )
@@ -285,9 +288,12 @@ def tile_allattentionpersistentmemoryheads_t_kernel(tc, q, k, v_bytes, v_scale, 
         ident_f32 = keep.tile([P, P], F32)
         make_identity(nc, ident_f32[:])
 
-        turn_qk(0)
+        turn_q(0)
+        turn_k(0)
         copy_qk(0)
-        km_bank = turn_rows(km_rows[:, 0], km_rows[:, 1])
+        km_bank = psum.tile([P, H * PACK, P], BF16, name="rows_bank")
+        for h in range(H):
+            turn_rows(km_bank, h, km_rows[:, h])
         km_t = keep.tile([P, H * PACK, P], BF16)
         nc.scalar.copy(out=km_t[:], in_=km_bank[:])
 
@@ -316,50 +322,53 @@ def tile_allattentionpersistentmemoryheads_t_kernel(tc, q, k, v_bytes, v_scale, 
                     scales=vm_scales[:],
                     in_=vm_inter[:].rearrange("p h e t -> p (h e t)"),
                 )
-            reciprocals(g - 1)
+            reciprocals(g - 1, 0)
             weigh_on_pool(g - 1)
-            spread_gates(g - 1)
-            turn_probs(g - 2, 3)
-            turn_qk(g + 1)
-            copy_probs(g - 2, 2)
-            copy_qk(g + 1)
-            turn_probs(g - 2, 0)
             copy_probs(g - 2, 3)
-            mix_values(g - 3)
+            exponentials(g - 1, 3)
+            spread_gates(g - 1)
+            turn_probs(g - 2, 0)
             turn_probs(g - 2, 1)
+            mix_values(g - 3)
             copy_probs(g - 2, 0)
-            store(g - 3)
             copy_probs(g - 2, 1)
+            store(g - 3)
 
             scan_logits(g, 0, 0)
             logits(g, 2, 0)
+            turn_q(g + 1)
             scan_logits(g, 1, 0)
             logits(g, 1, 1)
+            turn_k(g + 1)
             scan_logits(g, 0, 1)
-            exponentials(g, 0)
             logits(g, 3, 0)
+            interleave_v(g - 2)
+            exponentials(g, 0)
+            copy_qk(g + 1)
+            reciprocals(g - 1, 1)
+            weigh_on_vector(g - 1, 0)
+            weigh_on_vector(g - 1, 1)
+            weigh_on_vector(g - 1, 2)
+            turn_probs(g - 1, 2)
+            copy_probs(g - 1, 2)
             scan_logits(g, 2, 0)
             logits(g, 2, 1)
             scan_logits(g, 1, 1)
             logits(g, 3, 1)
-            interleave_v(g - 2)
+            exponentials(g, 1)
             if g == 0:
                 for h in range(H):
                     nc.scalar.copy(out=vm_inter[:, h], in_=vm_rows[:, h].rearrange("p t e -> p e t"))
                 widen_v(0)
                 widen_v(1)
             widen_v(g + 2)
-            exponentials(g, 1)
+            copy_v(g - 2)
             scan_logits(g, 3, 0)
             logits(g + 1, 0, 0)
+            weigh_on_vector(g - 1, 3)
+            turn_probs(g - 1, 3)
             scan_logits(g, 2, 1)
-            exponentials(g, 2)
             logits(g + 1, 1, 0)
-            weigh_on_vector(g - 1, 1)
-            weigh_on_vector(g - 1, 2)
-            turn_probs(g - 1, 2)
-            copy_v(g - 2)
+            exponentials(g, 2)
             scan_logits(g, 3, 1)
             logits(g + 1, 0, 1)
-            exponentials(g, 3)
-            weigh_on_vector(g - 1, 3)

@@ -21,7 +21,7 @@ KEYS = 2 * S
 GROUPS = B * H
 TILES = S // P
 V_BATCH = 4
-POOL_COLS = 896
+POOL_COLS = 1024
 POOL_COLS_LAST = 384
 
 
@@ -37,7 +37,7 @@ def tile_allattentionpersistentmemoryheads_t_kernel(tc, q, k, v_bytes, v_scale, 
         q_rows, k_rows, v_raw, qk_t, v_wide, v_inter = {}, {}, {}, {}, {}, {}
         banks, neg_logits, neg_max, sums, recips, exps, probs = {}, {}, {}, {}, {}, {}, {}
         turned, probs_t, p_codes, p_scales, v_codes, v_scales, gate_bank = {}, {}, {}, {}, {}, {}, {}
-        bank_count = []
+        bank_count, widened = [], []
 
         def live(g):
             return 0 <= g < GROUPS
@@ -59,7 +59,7 @@ def tile_allattentionpersistentmemoryheads_t_kernel(tc, q, k, v_bytes, v_scale, 
             if live(g):
                 n, b = divmod(g, V_BATCH)
                 if b == 0:
-                    v_raw[n] = work.tile([P, PACK, V_BATCH, E], U8, name="v_raw", align_bytes=64)
+                    v_raw[n] = work.tile([P, PACK, V_BATCH, E], U8, name="v_raw", bufs=4, align_bytes=64)
                 nc.sync.dma_start(
                     out=v_raw[n][:, :, b, :], in_=v_bytes[batch(g), head(g)].rearrange("(p t) e -> p t e", t=PACK)
                 )
@@ -164,7 +164,7 @@ def tile_allattentionpersistentmemoryheads_t_kernel(tc, q, k, v_bytes, v_scale, 
                 )
 
         def weigh_on_vector(g, i):
-            if live(g):
+            if live(g) and (i >= 2 or pool_cols(g) < KEYS):
                 cols = slice(pool_cols(g) if i < 2 else 0, KEYS)
                 nc.vector.scalar_tensor_tensor(
                     out=probs[g, i // 2][:, i % 2, cols],
@@ -192,11 +192,12 @@ def tile_allattentionpersistentmemoryheads_t_kernel(tc, q, k, v_bytes, v_scale, 
                     in_=turned["p", g, i][:].rearrange("p (c u) q -> p c q u", u=2),
                 )
 
-        def widen_v(step):
-            n, t = divmod(step, PACK)
+        def widen_v():
+            n, t = divmod(len(widened), PACK)
+            widened.append(1)
             if live(n * V_BATCH):
                 if t == 0:
-                    v_wide[n] = work.tile([P, PACK, V_BATCH, E], BF16, name="v_wide")
+                    v_wide[n] = work.tile([P, PACK, V_BATCH, E], BF16, name="v_wide", bufs=5)
                 nc.scalar.activation(
                     out=v_wide[n][:, t].rearrange("p b e -> p (b e)"),
                     in_=v_raw[n][:, t].rearrange("p b e -> p (b e)").bitcast(FP8),
@@ -220,15 +221,21 @@ def tile_allattentionpersistentmemoryheads_t_kernel(tc, q, k, v_bytes, v_scale, 
         def copy_v(g):
             if live(g):
                 v_inter[g] = work.tile([P, E, PACK], BF16, name="v_inter", align_bytes=64)
-                nc.scalar.copy(out=v_inter[g][:], in_=turned["v", g][:])
+                if g % 2 == 0:
+                    nc.scalar.copy(out=v_inter[g][:], in_=turned["v", g][:])
+                else:
+                    nc.vector.tensor_copy(out=v_inter[g][:], in_=turned["v", g][:])
 
         def quantize(g):
             if live(g):
                 p_codes[g] = work.tile([P, TILES * 2 * P], U32, name="p_codes", align_bytes=64)
                 p_scales[g] = work.tile([P, TILES * 2 * P], U8, name="p_scales", align_bytes=64)
+                nc.vector.quantize_mx(out=p_codes[g][:].bitcast(FP8X4), scales=p_scales[g][:], in_=probs_t[g][:])
+
+        def quantize_v(g):
+            if live(g):
                 v_codes[g] = work.tile([P, E], U32, name="v_codes", align_bytes=64)
                 v_scales[g] = work.tile([P, E], U8, name="v_scales", align_bytes=64)
-                nc.vector.quantize_mx(out=p_codes[g][:].bitcast(FP8X4), scales=p_scales[g][:], in_=probs_t[g][:])
                 nc.vector.quantize_mx(
                     out=v_codes[g][:].bitcast(FP8X4),
                     scales=v_scales[g][:],
@@ -264,6 +271,10 @@ def tile_allattentionpersistentmemoryheads_t_kernel(tc, q, k, v_bytes, v_scale, 
         nc.sync.dma_start(
             out=km_rows[:].rearrange("p h t e -> p h (t e)"), in_=km.rearrange("h (p t) e -> p h (t e)", t=PACK)
         )
+        scale_cols = keep.tile([P, PACK], F32)
+        nc.sync.dma_start(out=scale_cols[:], in_=v_scale.rearrange("a b (p t) c -> p (a b t c)", t=PACK))
+        for g in range(V_BATCH):
+            load_v(g)
         load_qk(1)
         gate_rows = []
         for name, row in (("tg_rows", tg), ("mg_rows", mg)):
@@ -274,9 +285,7 @@ def tile_allattentionpersistentmemoryheads_t_kernel(tc, q, k, v_bytes, v_scale, 
         nc.sync.dma_start(
             out=vm_rows[:].rearrange("p h t e -> p h (t e)"), in_=vm.rearrange("h (p t) e -> p h (t e)", t=PACK)
         )
-        scale_cols = keep.tile([P, PACK], F32)
-        nc.sync.dma_start(out=scale_cols[:], in_=v_scale.rearrange("a b (p t) c -> p (a b t c)", t=PACK))
-        for g in range(7):
+        for g in range(V_BATCH, 2 * V_BATCH):
             load_v(g)
 
         warm = keep.tile([P, 1], F32)
@@ -297,14 +306,21 @@ def tile_allattentionpersistentmemoryheads_t_kernel(tc, q, k, v_bytes, v_scale, 
         km_t = keep.tile([P, H * PACK, P], BF16)
         nc.scalar.copy(out=km_t[:], in_=km_bank[:])
 
+        for t in range(PACK):
+            widen_v()
+
+        def reorder_on_pool(dst, src):
+            nc.gpsimd.tensor_scalar(out=dst, in0=src, scalar1=1.0, scalar2=0.0, op0=ALU.mult, op1=ALU.add)
+
         gates = keep.tile([P, H, KEYS], BF16)
+        vm_inter = keep.tile([P, H, E, PACK], BF16, align_bytes=64)
         for h in range(H):
             for half in range(2):
-                nc.gpsimd.tensor_copy(
-                    out=gates[:, h, half * S : (half + 1) * S].rearrange("x (u p e) -> x u p e", u=2, e=2),
-                    in_=gate_rows[half][:, h * S : (h + 1) * S].rearrange("x (p u e) -> x u p e", u=2, e=2),
+                reorder_on_pool(
+                    gates[:, h, half * S : (half + 1) * S].rearrange("x (u p e) -> x u p e", u=2, e=2),
+                    gate_rows[half][:, h * S : (h + 1) * S].rearrange("x (p u e) -> x u p e", u=2, e=2),
                 )
-        vm_inter = keep.tile([P, H, E, PACK], BF16, align_bytes=64)
+            reorder_on_pool(vm_inter[:, h], vm_rows[:, h].rearrange("p t e -> p e t"))
         vm_codes = keep.tile([P, H * E], U32, align_bytes=64)
         vm_scales = keep.tile([P, H * E], U8, align_bytes=64)
 
@@ -314,9 +330,14 @@ def tile_allattentionpersistentmemoryheads_t_kernel(tc, q, k, v_bytes, v_scale, 
 
         for g in range(GROUPS + 3):
             load_qk(g + 2)
-            load_v(g + 7)
+            if g < 2:
+                for b in range(V_BATCH):
+                    load_v((g + 2) * V_BATCH + b)
+            else:
+                load_v(g + 14)
             quantize(g - 3)
-            if g == 1:
+            quantize_v(g - 2)
+            if g == 2:
                 nc.vector.quantize_mx(
                     out=vm_codes[:].bitcast(FP8X4),
                     scales=vm_scales[:],
@@ -340,12 +361,12 @@ def tile_allattentionpersistentmemoryheads_t_kernel(tc, q, k, v_bytes, v_scale, 
             scan_logits(g, 1, 0)
             logits(g, 1, 1)
             turn_k(g + 1)
+            reciprocals(g - 1, 1)
             scan_logits(g, 0, 1)
             logits(g, 3, 0)
-            interleave_v(g - 2)
+            interleave_v(g - 1)
             exponentials(g, 0)
             copy_qk(g + 1)
-            reciprocals(g - 1, 1)
             weigh_on_vector(g - 1, 0)
             weigh_on_vector(g - 1, 1)
             weigh_on_vector(g - 1, 2)
@@ -356,15 +377,11 @@ def tile_allattentionpersistentmemoryheads_t_kernel(tc, q, k, v_bytes, v_scale, 
             scan_logits(g, 1, 1)
             logits(g, 3, 1)
             exponentials(g, 1)
-            if g == 0:
-                for h in range(H):
-                    nc.scalar.copy(out=vm_inter[:, h], in_=vm_rows[:, h].rearrange("p t e -> p e t"))
-                widen_v(0)
-                widen_v(1)
-            widen_v(g + 2)
-            copy_v(g - 2)
+            for n in range(3 if g < 3 else 1):
+                widen_v()
             scan_logits(g, 3, 0)
             logits(g + 1, 0, 0)
+            copy_v(g - 1)
             weigh_on_vector(g - 1, 3)
             turn_probs(g - 1, 3)
             scan_logits(g, 2, 1)

@@ -20,9 +20,10 @@ PACK = 4
 KEYS = 2 * S
 GROUPS = B * H
 TILES = S // P
+LOGIT_BANKS = 3
 V_BATCH = 4
-POOL_COLS = 1024
-POOL_COLS_LAST = 384
+POOL_COLS = 1888
+POOL_COLS_LAST = 768
 
 
 def tile_allattentionpersistentmemoryheads_t_kernel(tc, q, k, v_bytes, v_scale, km, vm, tg, mg, out):
@@ -34,10 +35,10 @@ def tile_allattentionpersistentmemoryheads_t_kernel(tc, q, k, v_bytes, v_scale, 
         psum = ctx.enter_context(tc.psum_pool(name="psum", bufs=1))
         ctx.enter_context(tc.manual_schedule())
 
-        q_rows, k_rows, v_raw, qk_t, v_wide, v_inter = {}, {}, {}, {}, {}, {}
-        banks, neg_logits, neg_max, sums, recips, exps, probs = {}, {}, {}, {}, {}, {}, {}
-        turned, probs_t, p_codes, p_scales, v_codes, v_scales, gate_bank = {}, {}, {}, {}, {}, {}, {}
-        bank_count, widened = [], []
+        q_rows, k_rows, qk_bank, qk_t = {}, {}, {}, {}
+        logit_bank, neg_logits, neg_max, sums, recips, exps, probs = {}, {}, {}, {}, {}, {}, {}
+        gate_bank, probs_bank, probs_t, p_codes, p_scales = {}, {}, {}, {}, {}
+        v_raw, v_wide, v_bank, v_inter, v_codes, v_scales, out_bank = {}, {}, {}, {}, {}, {}, {}
 
         def live(g):
             return 0 <= g < GROUPS
@@ -50,8 +51,8 @@ def tile_allattentionpersistentmemoryheads_t_kernel(tc, q, k, v_bytes, v_scale, 
 
         def load_qk(g):
             if live(g):
-                q_rows[g] = work.tile([P, PACK, E], BF16, name="q_rows")
-                k_rows[g] = work.tile([P, PACK, E], BF16, name="k_rows")
+                q_rows[g] = work.tile([P, PACK, E], BF16, name="q_rows", bufs=4)
+                k_rows[g] = work.tile([P, PACK, E], BF16, name="k_rows", bufs=4)
                 nc.sync.dma_start(out=q_rows[g][:], in_=q[batch(g), head(g)].rearrange("(p t) e -> p t e", t=PACK))
                 nc.sync.dma_start(out=k_rows[g][:], in_=k[batch(g), head(g)].rearrange("(p t) e -> p t e", t=PACK))
 
@@ -59,34 +60,33 @@ def tile_allattentionpersistentmemoryheads_t_kernel(tc, q, k, v_bytes, v_scale, 
             if live(g):
                 n, b = divmod(g, V_BATCH)
                 if b == 0:
-                    v_raw[n] = work.tile([P, PACK, V_BATCH, E], U8, name="v_raw", bufs=4, align_bytes=64)
+                    v_raw[n] = work.tile([P, PACK, V_BATCH, E], U8, name="v_raw", align_bytes=64)
                 nc.sync.dma_start(
                     out=v_raw[n][:, :, b, :], in_=v_bytes[batch(g), head(g)].rearrange("(p t) e -> p t e", t=PACK)
                 )
 
-        def turn_rows(bank, n, rows):
+        def turn_rows(bank, slot, rows):
             for t in range(PACK):
-                nc.tensor.transpose(bank[:, n * PACK + t, :], rows[:, t, :], ident_bf16[:])
+                nc.tensor.transpose(bank[:, slot * PACK + t, :], rows[:, t, :], ident_bf16[:])
 
         def turn_q(g):
             if live(g):
-                turned["qk", g] = psum.tile([P, 2 * PACK, P], BF16, name="rows_bank")
-                turn_rows(turned["qk", g], 0, q_rows[g])
+                qk_bank[g] = psum.tile([P, 2 * PACK, P], BF16, name="rows_bank")
+                turn_rows(qk_bank[g], 0, q_rows[g])
 
         def turn_k(g):
             if live(g):
-                turn_rows(turned["qk", g], 1, k_rows[g])
+                turn_rows(qk_bank[g], 1, k_rows[g])
 
         def copy_qk(g):
             if live(g):
                 qk_t[g] = work.tile([P, 2 * PACK, P], BF16, name="qk_t")
-                nc.scalar.copy(out=qk_t[g][:], in_=turned["qk", g][:])
+                nc.scalar.copy(out=qk_t[g][:], in_=qk_bank[g][:])
 
         def logits(g, i, half):
             if live(g):
-                bank = psum.tile([P, S], F32, name="logit_bank%d" % (len(bank_count) % 3))
-                bank_count.append(1)
-                banks[g, i, half] = bank
+                bank = psum.tile([P, S], F32, name="logit_bank%d" % (len(logit_bank) % LOGIT_BANKS))
+                logit_bank[g, i, half] = bank
                 if half == 0:
                     keys = qk_t[g][:, PACK:, :]
                 else:
@@ -96,20 +96,19 @@ def tile_allattentionpersistentmemoryheads_t_kernel(tc, q, k, v_bytes, v_scale, 
                 )
 
         def scan_logits(g, i, half):
-            if live(g):
-                if half == 0:
-                    neg_logits[g, i] = work.tile([P, KEYS], F32, name="neg_logits", bufs=5)
-                    if i == 0:
-                        neg_max[g] = work.tile([P, TILES, 2], F32, name="neg_max")
-                nc.vector.tensor_scalar(
-                    out=neg_logits[g, i][:, half * S : (half + 1) * S].rearrange("q (u p e) -> q u p e", u=2, e=2),
-                    in0=banks[g, i, half][:].rearrange("q (u e p) -> q u p e", u=2, e=2),
-                    scalar1=-1.0,
-                    scalar2=None if half == 0 else neg_max[g][:, i, 0:1],
-                    op0=ALU.mult,
-                    op1=ALU.min,
-                    accum_out=neg_max[g][:, i, half : half + 1],
-                )
+            if half == 0:
+                neg_logits[g, i] = work.tile([P, KEYS], F32, name="neg_logits", bufs=5)
+                if i == 0:
+                    neg_max[g] = work.tile([P, TILES, 2], F32, name="neg_max")
+            nc.vector.tensor_scalar(
+                out=neg_logits[g, i][:, half * S : (half + 1) * S].rearrange("q (u p e) -> q u p e", u=2, e=2),
+                in0=logit_bank[g, i, half][:].rearrange("q (u e p) -> q u p e", u=2, e=2),
+                scalar1=-1.0,
+                scalar2=None if half == 0 else neg_max[g][:, i, 0:1],
+                op0=ALU.mult,
+                op1=ALU.min,
+                accum_out=neg_max[g][:, i, half : half + 1],
+            )
 
         def exponentials(g, i):
             if live(g):
@@ -138,34 +137,38 @@ def tile_allattentionpersistentmemoryheads_t_kernel(tc, q, k, v_bytes, v_scale, 
                 for half in range(2):
                     cols = slice(half * S, (half + 1) * S)
                     nc.tensor.matmul(
-                        out=bank[:, cols], lhsT=ident_bf16[:], rhs=gates[:, head(g), cols], start=True, stop=True
+                        out=bank[:, cols], lhsT=ident_bf16[:], rhs=gates[:, head(g), 0, cols], start=True, stop=True
                     )
 
-        def pool_cols(g):
-            return POOL_COLS_LAST if g == GROUPS - 1 else POOL_COLS
+        def pool_cols(g, i):
+            share = POOL_COLS_LAST if g == GROUPS - 1 else POOL_COLS
+            return min(max(share - i * KEYS, 0), KEYS)
 
         def weigh_on_pool(g):
             if live(g):
-                pair, n = exps[g, 0], pool_cols(g)
+                pair = exps[g, 0]
                 for i in range(2):
-                    nc.gpsimd.tensor_scalar(
-                        out=pair[:, i, :n],
-                        in0=pair[:, i, :n],
-                        scalar1=recips[g, 0][:, i : i + 1],
-                        scalar2=0.0,
-                        op0=ALU.mult,
-                        op1=ALU.add,
-                    )
+                    width = pool_cols(g, i)
+                    if width > 0:
+                        nc.gpsimd.tensor_scalar(
+                            out=pair[:, i, :width],
+                            in0=pair[:, i, :width],
+                            scalar1=recips[g, 0][:, i : i + 1],
+                            scalar2=0.0,
+                            op0=ALU.mult,
+                            op1=ALU.add,
+                        )
+                total = pool_cols(g, 0) + pool_cols(g, 1)
                 nc.gpsimd.tensor_tensor(
-                    out=probs[g, 0][:, :, :n],
-                    in0=pair[:, :, :n],
-                    in1=gates[:, head(g), :n].unsqueeze(1).to_broadcast([P, 2, n]),
+                    out=probs[g, 0][:].rearrange("q i c -> q (i c)")[:, :total],
+                    in0=pair[:].rearrange("q i c -> q (i c)")[:, :total],
+                    in1=gates[:, head(g)].rearrange("q i c -> q (i c)")[:, :total],
                     op=ALU.mult,
                 )
 
         def weigh_on_vector(g, i):
-            if live(g) and (i >= 2 or pool_cols(g) < KEYS):
-                cols = slice(pool_cols(g) if i < 2 else 0, KEYS)
+            if live(g):
+                cols = slice(pool_cols(g, i), KEYS)
                 nc.vector.scalar_tensor_tensor(
                     out=probs[g, i // 2][:, i % 2, cols],
                     in0=exps[g, i // 2][:, i % 2, cols],
@@ -175,29 +178,28 @@ def tile_allattentionpersistentmemoryheads_t_kernel(tc, q, k, v_bytes, v_scale, 
                     op1=ALU.mult,
                 )
 
-        def turn_probs(g, i):
+        def turn_probs(g, i, bank_name=None):
             if live(g):
-                bank = psum.tile([P, PACK, P], F32, name="probs_bank%d" % (i % 2))
-                turned["p", g, i] = bank
+                bank = psum.tile([P, PACK, P], F32, name=bank_name or "probs_bank%d" % (i % 2))
+                probs_bank[g, i] = bank
                 words = probs[g, i // 2][:, i % 2, :].bitcast(F32)
                 for n in range(PACK):
                     nc.tensor.transpose(bank[:, n, :], words[:, n * P : (n + 1) * P], ident_f32[:])
 
-        def copy_probs(g, i):
+        def copy_probs(g, i, copy=nc.scalar.copy):
             if live(g):
-                if i == 2:
+                if g not in probs_t:
                     probs_t[g] = work.tile([P, TILES * KEYS], BF16, name="probs_t", align_bytes=64)
-                nc.scalar.copy(
+                copy(
                     out=probs_t[g][:, i * KEYS : (i + 1) * KEYS].bitcast(F32).rearrange("p (c q u) -> p c q u", c=2, u=2),
-                    in_=turned["p", g, i][:].rearrange("p (c u) q -> p c q u", u=2),
+                    in_=probs_bank[g, i][:].rearrange("p (c u) q -> p c q u", u=2),
                 )
 
-        def widen_v():
-            n, t = divmod(len(widened), PACK)
-            widened.append(1)
+        def widen_v(step):
+            n, t = divmod(step, PACK)
             if live(n * V_BATCH):
                 if t == 0:
-                    v_wide[n] = work.tile([P, PACK, V_BATCH, E], BF16, name="v_wide", bufs=5)
+                    v_wide[n] = work.tile([P, PACK, V_BATCH, E], BF16, name="v_wide")
                 nc.scalar.activation(
                     out=v_wide[n][:, t].rearrange("p b e -> p (b e)"),
                     in_=v_raw[n][:, t].rearrange("p b e -> p (b e)").bitcast(FP8),
@@ -205,28 +207,23 @@ def tile_allattentionpersistentmemoryheads_t_kernel(tc, q, k, v_bytes, v_scale, 
                     scale=scale_cols[:, t : t + 1],
                 )
 
-        def interleave_v(g):
+        def interleave(bank, rows):
+            nc.tensor.matmul(
+                out=bank, lhsT=ident_bf16[:], rhs=rows.rearrange("p t e -> p e t"), start=True, stop=True
+            )
+
+        def interleave_v(g, bank_name="out_bank"):
             if live(g):
                 n, b = divmod(g, V_BATCH)
-                bank = psum.tile([P, E, PACK], BF16, name="out_bank")
-                turned["v", g] = bank
-                nc.tensor.matmul(
-                    out=bank[:],
-                    lhsT=ident_bf16[:],
-                    rhs=v_wide[n][:, :, b, :].rearrange("p t e -> p e t"),
-                    start=True,
-                    stop=True,
-                )
+                v_bank[g] = psum.tile([P, E, PACK], BF16, name=bank_name)
+                interleave(v_bank[g][:], v_wide[n][:, :, b, :])
 
         def copy_v(g):
             if live(g):
                 v_inter[g] = work.tile([P, E, PACK], BF16, name="v_inter", align_bytes=64)
-                if g % 2 == 0:
-                    nc.scalar.copy(out=v_inter[g][:], in_=turned["v", g][:])
-                else:
-                    nc.vector.tensor_copy(out=v_inter[g][:], in_=turned["v", g][:])
+                nc.scalar.copy(out=v_inter[g][:], in_=v_bank[g][:])
 
-        def quantize(g):
+        def quantize_probs(g):
             if live(g):
                 p_codes[g] = work.tile([P, TILES * 2 * P], U32, name="p_codes", align_bytes=64)
                 p_scales[g] = work.tile([P, TILES * 2 * P], U8, name="p_scales", align_bytes=64)
@@ -244,13 +241,13 @@ def tile_allattentionpersistentmemoryheads_t_kernel(tc, q, k, v_bytes, v_scale, 
 
         def mix_values(g):
             if live(g):
-                bank = psum.tile([P, TILES, E], F32, name="out_bank")
+                out_bank[g] = psum.tile([P, TILES, E], F32, name="out_bank")
                 mem = slice(head(g) * E, (head(g) + 1) * E)
                 for i in range(TILES):
                     for half in range(2):
                         cols = slice((2 * i + half) * P, (2 * i + half + 1) * P)
                         nc.tensor.matmul_mx(
-                            out=bank[:, i, :],
+                            out=out_bank[g][:, i, :],
                             lhsT=p_codes[g][:, cols].bitcast(FP8X4),
                             lhsT_scale=p_scales[g][:, cols],
                             rhs=(v_codes[g][:] if half == 0 else vm_codes[:, mem]).bitcast(FP8X4),
@@ -258,12 +255,11 @@ def tile_allattentionpersistentmemoryheads_t_kernel(tc, q, k, v_bytes, v_scale, 
                             start=(half == 0),
                             stop=(half == 1),
                         )
-                turned["out", g] = bank
 
         def store(g):
             if live(g):
                 result = work.tile([P, TILES, E], F32, name="result")
-                nc.scalar.copy(out=result[:], in_=turned["out", g][:])
+                nc.scalar.copy(out=result[:], in_=out_bank[g][:])
                 nc.sync.dma_start(out=out[batch(g), head(g)].rearrange("(p t) e -> p t e", t=PACK), in_=result[:])
 
         load_qk(0)
@@ -277,10 +273,10 @@ def tile_allattentionpersistentmemoryheads_t_kernel(tc, q, k, v_bytes, v_scale, 
             load_v(g)
         load_qk(1)
         gate_rows = []
-        for name, row in (("tg_rows", tg), ("mg_rows", mg)):
-            rows = keep.tile([P, H * S], BF16, name=name)
-            nc.sync.dma_start(out=rows[:], in_=row.rearrange("h s -> (h s)").partition_broadcast(P))
-            gate_rows.append(rows)
+        for name, gate in (("tg_rows", tg), ("mg_rows", mg)):
+            spread = keep.tile([P, H * S], BF16, name=name)
+            nc.sync.dma_start(out=spread[:], in_=gate.rearrange("h s -> (h s)").partition_broadcast(P))
+            gate_rows.append(spread)
         vm_rows = keep.tile([P, H, PACK, E], BF16)
         nc.sync.dma_start(
             out=vm_rows[:].rearrange("p h t e -> p h (t e)"), in_=vm.rearrange("h (p t) e -> p h (t e)", t=PACK)
@@ -299,43 +295,42 @@ def tile_allattentionpersistentmemoryheads_t_kernel(tc, q, k, v_bytes, v_scale, 
 
         turn_q(0)
         turn_k(0)
-        copy_qk(0)
-        km_bank = psum.tile([P, H * PACK, P], BF16, name="rows_bank")
+        km_bank = psum.tile([P, H * PACK, P], BF16, name="out_bank")
         for h in range(H):
             turn_rows(km_bank, h, km_rows[:, h])
         km_t = keep.tile([P, H * PACK, P], BF16)
-        nc.scalar.copy(out=km_t[:], in_=km_bank[:])
+        copy_qk(0)
+        nc.vector.tensor_copy(out=km_t[:], in_=km_bank[:])
 
         for t in range(PACK):
-            widen_v()
+            widen_v(t)
 
-        def reorder_on_pool(dst, src):
-            nc.gpsimd.tensor_scalar(out=dst, in0=src, scalar1=1.0, scalar2=0.0, op0=ALU.mult, op1=ALU.add)
-
-        gates = keep.tile([P, H, KEYS], BF16)
+        gates = keep.tile([P, H, 2, KEYS], BF16)
         vm_inter = keep.tile([P, H, E, PACK], BF16, align_bytes=64)
         for h in range(H):
             for half in range(2):
-                reorder_on_pool(
-                    gates[:, h, half * S : (half + 1) * S].rearrange("x (u p e) -> x u p e", u=2, e=2),
-                    gate_rows[half][:, h * S : (h + 1) * S].rearrange("x (p u e) -> x u p e", u=2, e=2),
+                nc.gpsimd.tensor_scalar(
+                    out=gates[:, h, 0, half * S : (half + 1) * S].rearrange("x (u p e) -> x u p e", u=2, e=2),
+                    in0=gate_rows[half][:, h * S : (h + 1) * S].rearrange("x (p u e) -> x u p e", u=2, e=2),
+                    scalar1=1.0,
+                    scalar2=0.0,
+                    op0=ALU.mult,
+                    op1=ALU.add,
                 )
-            reorder_on_pool(vm_inter[:, h], vm_rows[:, h].rearrange("p t e -> p e t"))
         vm_codes = keep.tile([P, H * E], U32, align_bytes=64)
         vm_scales = keep.tile([P, H * E], U8, align_bytes=64)
 
         logits(0, 0, 0)
         logits(0, 1, 0)
         logits(0, 0, 1)
+        load_qk(2)
+        turn_q(1)
+        turn_k(1)
 
-        for g in range(GROUPS + 3):
-            load_qk(g + 2)
-            if g < 2:
-                for b in range(V_BATCH):
-                    load_v((g + 2) * V_BATCH + b)
-            else:
-                load_v(g + 14)
-            quantize(g - 3)
+        for g in range(GROUPS):
+            load_qk(g + 3)
+            load_v(g + 2 * V_BATCH)
+            quantize_probs(g - 3)
             quantize_v(g - 2)
             if g == 2:
                 nc.vector.quantize_mx(
@@ -343,6 +338,8 @@ def tile_allattentionpersistentmemoryheads_t_kernel(tc, q, k, v_bytes, v_scale, 
                     scales=vm_scales[:],
                     in_=vm_inter[:].rearrange("p h e t -> p (h e t)"),
                 )
+            if g == 1:
+                nc.vector.tensor_copy(out=gates[:, :, 1, :], in_=gates[:, :, 0, :])
             reciprocals(g - 1, 0)
             weigh_on_pool(g - 1)
             copy_probs(g - 2, 3)
@@ -354,20 +351,23 @@ def tile_allattentionpersistentmemoryheads_t_kernel(tc, q, k, v_bytes, v_scale, 
             copy_probs(g - 2, 0)
             copy_probs(g - 2, 1)
             store(g - 3)
+            if g == 1:
+                vm_bank = psum.tile([P, H, E, PACK], BF16, name="out_bank")
+                for h in range(H):
+                    interleave(vm_bank[:, h], vm_rows[:, h])
+                nc.scalar.copy(out=vm_inter[:], in_=vm_bank[:])
 
             scan_logits(g, 0, 0)
             logits(g, 2, 0)
-            turn_q(g + 1)
             scan_logits(g, 1, 0)
             logits(g, 1, 1)
-            turn_k(g + 1)
-            reciprocals(g - 1, 1)
             scan_logits(g, 0, 1)
             logits(g, 3, 0)
-            interleave_v(g - 1)
             exponentials(g, 0)
             copy_qk(g + 1)
-            weigh_on_vector(g - 1, 0)
+            if g > 0:
+                widen_v(PACK + g - 1)
+            reciprocals(g - 1, 1)
             weigh_on_vector(g - 1, 1)
             weigh_on_vector(g - 1, 2)
             turn_probs(g - 1, 2)
@@ -377,15 +377,52 @@ def tile_allattentionpersistentmemoryheads_t_kernel(tc, q, k, v_bytes, v_scale, 
             scan_logits(g, 1, 1)
             logits(g, 3, 1)
             exponentials(g, 1)
-            for n in range(3 if g < 3 else 1):
-                widen_v()
             scan_logits(g, 3, 0)
             logits(g + 1, 0, 0)
-            copy_v(g - 1)
+            interleave_v(g - 1)
+            turn_q(g + 2)
             weigh_on_vector(g - 1, 3)
             turn_probs(g - 1, 3)
             scan_logits(g, 2, 1)
             logits(g + 1, 1, 0)
+            turn_k(g + 2)
             exponentials(g, 2)
             scan_logits(g, 3, 1)
             logits(g + 1, 0, 1)
+            copy_v(g - 1)
+
+        last = GROUPS - 1
+        quantize_probs(last - 2)
+        quantize_v(last - 1)
+        reciprocals(last, 0)
+        weigh_on_pool(last)
+        weigh_on_vector(last, 0)
+        weigh_on_vector(last, 1)
+        copy_probs(last - 1, 3)
+        exponentials(last, 3)
+        turn_probs(last - 1, 0)
+        turn_probs(last - 1, 1)
+        mix_values(last - 2)
+        copy_probs(last - 1, 0)
+        copy_probs(last - 1, 1)
+        store(last - 2)
+        interleave_v(last, "rows_bank")
+        copy_v(last)
+        reciprocals(last, 1)
+        weigh_on_vector(last, 2)
+        weigh_on_vector(last, 3)
+        turn_probs(last, 2)
+        turn_probs(last, 1)
+        turn_probs(last, 0, "logit_bank0")
+        turn_probs(last, 3, "logit_bank1")
+        quantize_probs(last - 1)
+        copy_probs(last, 2)
+        copy_probs(last, 1)
+        copy_probs(last, 0)
+        copy_probs(last, 3, nc.vector.tensor_copy)
+        quantize_v(last)
+        mix_values(last - 1)
+        quantize_probs(last)
+        store(last - 1)
+        mix_values(last)
+        store(last)

from contextlib import ExitStack

import concourse.mybir as mybir
from concourse.masks import make_identity

B, H, S, E = 16, 2, 512, 128
FLOPS = 2 * 2 * B * H * S * (2 * S) * E

F32 = mybir.dt.float32
BF16 = mybir.dt.bfloat16
U32 = mybir.dt.uint32
U8 = mybir.dt.uint8
FP8 = mybir.dt.float8_e4m3fn
FP8X4 = mybir.dt.float8_e4m3fn_x4
ALU = mybir.AluOpType
ACT = mybir.ActivationFunctionType

P = 128
PACK = 4
KEYS = 2 * S
GROUPS = B * H
TILES = S // P
LOGIT_BANKS = 3
V_BATCH = 4
POOL_COLS = 1888
POOL_COLS_LAST = 768


def tile_allattentionpersistentmemoryheads_t_kernel(tc, q, k, v_bytes, v_scale, km, vm, tg, mg, out):
    nc = tc.nc

    with ExitStack() as ctx:
        keep = ctx.enter_context(tc.tile_pool(name="keep", bufs=1))
        work = ctx.enter_context(tc.tile_pool(name="work", bufs=3))
        psum = ctx.enter_context(tc.psum_pool(name="psum", bufs=1))
        ctx.enter_context(tc.manual_schedule())

        q_rows, k_rows, qk_bank, qk_t = {}, {}, {}, {}
        logit_bank, neg_logits, neg_max, sums, recips, exps, probs = {}, {}, {}, {}, {}, {}, {}
        gate_bank, probs_bank, probs_t, p_codes, p_scales = {}, {}, {}, {}, {}
        v_raw, v_wide, v_bank, v_inter, v_codes, v_scales, out_bank = {}, {}, {}, {}, {}, {}, {}

        def live(g):
            return 0 <= g < GROUPS

        def head(g):
            return g // B

        def batch(g):
            return g % B

        def load_qk(g):
            if live(g):
                q_rows[g] = work.tile([P, PACK, E], BF16, name="q_rows", bufs=4)
                k_rows[g] = work.tile([P, PACK, E], BF16, name="k_rows", bufs=4)
                nc.sync.dma_start(out=q_rows[g][:], in_=q[batch(g), head(g)].rearrange("(p t) e -> p t e", t=PACK))
                nc.sync.dma_start(out=k_rows[g][:], in_=k[batch(g), head(g)].rearrange("(p t) e -> p t e", t=PACK))

        def load_v(g):
            if live(g):
                n, b = divmod(g, V_BATCH)
                if b == 0:
                    v_raw[n] = work.tile([P, PACK, V_BATCH, E], U8, name="v_raw", align_bytes=64)
                nc.sync.dma_start(
                    out=v_raw[n][:, :, b, :], in_=v_bytes[batch(g), head(g)].rearrange("(p t) e -> p t e", t=PACK)
                )

        def turn_rows(bank, slot, rows):
            for t in range(PACK):
                nc.tensor.transpose(bank[:, slot * PACK + t, :], rows[:, t, :], ident_bf16[:])

        def turn_q(g):
            if live(g):
                qk_bank[g] = psum.tile([P, 2 * PACK, P], BF16, name="rows_bank")
                turn_rows(qk_bank[g], 0, q_rows[g])

        def turn_k(g):
            if live(g):
                turn_rows(qk_bank[g], 1, k_rows[g])

        def copy_qk(g):
            if live(g):
                qk_t[g] = work.tile([P, 2 * PACK, P], BF16, name="qk_t")
                nc.scalar.copy(out=qk_t[g][:], in_=qk_bank[g][:])

        def logits(g, i, half):
            if live(g):
                bank = psum.tile([P, S], F32, name="logit_bank%d" % (len(logit_bank) % LOGIT_BANKS))
                logit_bank[g, i, half] = bank
                if half == 0:
                    keys = qk_t[g][:, PACK:, :]
                else:
                    keys = km_t[:, head(g) * PACK : (head(g) + 1) * PACK, :]
                nc.tensor.matmul(
                    out=bank[:], lhsT=qk_t[g][:, i, :], rhs=keys.rearrange("e t p -> e (t p)"), start=True, stop=True
                )

        def scan_logits(g, i, half):
            if half == 0:
                neg_logits[g, i] = work.tile([P, KEYS], F32, name="neg_logits", bufs=5)
                if i == 0:
                    neg_max[g] = work.tile([P, TILES, 2], F32, name="neg_max")
            nc.vector.tensor_scalar(
                out=neg_logits[g, i][:, half * S : (half + 1) * S].rearrange("q (u p e) -> q u p e", u=2, e=2),
                in0=logit_bank[g, i, half][:].rearrange("q (u e p) -> q u p e", u=2, e=2),
                scalar1=-1.0,
                scalar2=None if half == 0 else neg_max[g][:, i, 0:1],
                op0=ALU.mult,
                op1=ALU.min,
                accum_out=neg_max[g][:, i, half : half + 1],
            )

        def exponentials(g, i):
            if live(g):
                if i % 2 == 0:
                    sums[g, i // 2] = work.tile([P, 2], F32, name="sums", bufs=4)
                    exps[g, i // 2] = work.tile([P, 2, KEYS], F32, name="exps", bufs=5)
                nc.scalar.activation(
                    out=exps[g, i // 2][:, i % 2, :],
                    in_=neg_logits[g, i][:],
                    func=ACT.Exp,
                    bias=neg_max[g][:, i, 1:2],
                    scale=-1.0,
                    accum_out=sums[g, i // 2][:, i % 2 : i % 2 + 1],
                )

        def reciprocals(g, pair):
            if live(g):
                recips[g, pair] = work.tile([P, 2], F32, name="recips", bufs=4)
                nc.vector.reciprocal(out=recips[g, pair][:], in_=sums[g, pair][:])
                probs[g, pair] = work.tile([P, 2, KEYS], BF16, name="probs", bufs=5, align_bytes=64)

        def spread_gates(g):
            if live(g) and batch(g) == 0:
                bank = psum.tile([P, KEYS], BF16, name="gate_bank")
                gate_bank[head(g)] = bank
                for half in range(2):
                    cols = slice(half * S, (half + 1) * S)
                    nc.tensor.matmul(
                        out=bank[:, cols], lhsT=ident_bf16[:], rhs=gates[:, head(g), 0, cols], start=True, stop=True
                    )

        def pool_cols(g, i):
            share = POOL_COLS_LAST if g == GROUPS - 1 else POOL_COLS
            return min(max(share - i * KEYS, 0), KEYS)

        def weigh_on_pool(g):
            if live(g):
                pair = exps[g, 0]
                for i in range(2):
                    width = pool_cols(g, i)
                    if width > 0:
                        nc.gpsimd.tensor_scalar(
                            out=pair[:, i, :width],
                            in0=pair[:, i, :width],
                            scalar1=recips[g, 0][:, i : i + 1],
                            scalar2=0.0,
                            op0=ALU.mult,
                            op1=ALU.add,
                        )
                total = pool_cols(g, 0) + pool_cols(g, 1)
                nc.gpsimd.tensor_tensor(
                    out=probs[g, 0][:].rearrange("q i c -> q (i c)")[:, :total],
                    in0=pair[:].rearrange("q i c -> q (i c)")[:, :total],
                    in1=gates[:, head(g)].rearrange("q i c -> q (i c)")[:, :total],
                    op=ALU.mult,
                )

        def weigh_on_vector(g, i):
            if live(g):
                cols = slice(pool_cols(g, i), KEYS)
                nc.vector.scalar_tensor_tensor(
                    out=probs[g, i // 2][:, i % 2, cols],
                    in0=exps[g, i // 2][:, i % 2, cols],
                    scalar=recips[g, i // 2][:, i % 2 : i % 2 + 1],
                    in1=gate_bank[head(g)][:, cols],
                    op0=ALU.mult,
                    op1=ALU.mult,
                )

        def turn_probs(g, i, bank_name=None):
            if live(g):
                bank = psum.tile([P, PACK, P], F32, name=bank_name or "probs_bank%d" % (i % 2))
                probs_bank[g, i] = bank
                words = probs[g, i // 2][:, i % 2, :].bitcast(F32)
                for n in range(PACK):
                    nc.tensor.transpose(bank[:, n, :], words[:, n * P : (n + 1) * P], ident_f32[:])

        def copy_probs(g, i, copy=nc.scalar.copy):
            if live(g):
                if g not in probs_t:
                    probs_t[g] = work.tile([P, TILES * KEYS], BF16, name="probs_t", align_bytes=64)
                copy(
                    out=probs_t[g][:, i * KEYS : (i + 1) * KEYS].bitcast(F32).rearrange("p (c q u) -> p c q u", c=2, u=2),
                    in_=probs_bank[g, i][:].rearrange("p (c u) q -> p c q u", u=2),
                )

        def widen_v(step):
            n, t = divmod(step, PACK)
            if live(n * V_BATCH):
                if t == 0:
                    v_wide[n] = work.tile([P, PACK, V_BATCH, E], BF16, name="v_wide")
                nc.scalar.activation(
                    out=v_wide[n][:, t].rearrange("p b e -> p (b e)"),
                    in_=v_raw[n][:, t].rearrange("p b e -> p (b e)").bitcast(FP8),
                    func=ACT.Copy,
                    scale=scale_cols[:, t : t + 1],
                )

        def interleave(bank, rows):
            nc.tensor.matmul(
                out=bank, lhsT=ident_bf16[:], rhs=rows.rearrange("p t e -> p e t"), start=True, stop=True
            )

        def interleave_v(g, bank_name="out_bank"):
            if live(g):
                n, b = divmod(g, V_BATCH)
                v_bank[g] = psum.tile([P, E, PACK], BF16, name=bank_name)
                interleave(v_bank[g][:], v_wide[n][:, :, b, :])

        def copy_v(g):
            if live(g):
                v_inter[g] = work.tile([P, E, PACK], BF16, name="v_inter", align_bytes=64)
                nc.scalar.copy(out=v_inter[g][:], in_=v_bank[g][:])

        def quantize_probs(g):
            if live(g):
                p_codes[g] = work.tile([P, TILES * 2 * P], U32, name="p_codes", align_bytes=64)
                p_scales[g] = work.tile([P, TILES * 2 * P], U8, name="p_scales", align_bytes=64)
                nc.vector.quantize_mx(out=p_codes[g][:].bitcast(FP8X4), scales=p_scales[g][:], in_=probs_t[g][:])

        def quantize_v(g):
            if live(g):
                v_codes[g] = work.tile([P, E], U32, name="v_codes", align_bytes=64)
                v_scales[g] = work.tile([P, E], U8, name="v_scales", align_bytes=64)
                nc.vector.quantize_mx(
                    out=v_codes[g][:].bitcast(FP8X4),
                    scales=v_scales[g][:],
                    in_=v_inter[g][:].rearrange("p e t -> p (e t)"),
                )

        def mix_values(g):
            if live(g):
                out_bank[g] = psum.tile([P, TILES, E], F32, name="out_bank")
                mem = slice(head(g) * E, (head(g) + 1) * E)
                for i in range(TILES):
                    for half in range(2):
                        cols = slice((2 * i + half) * P, (2 * i + half + 1) * P)
                        nc.tensor.matmul_mx(
                            out=out_bank[g][:, i, :],
                            lhsT=p_codes[g][:, cols].bitcast(FP8X4),
                            lhsT_scale=p_scales[g][:, cols],
                            rhs=(v_codes[g][:] if half == 0 else vm_codes[:, mem]).bitcast(FP8X4),
                            rhs_scale=v_scales[g][:] if half == 0 else vm_scales[:, mem],
                            start=(half == 0),
                            stop=(half == 1),
                        )

        def store(g):
            if live(g):
                result = work.tile([P, TILES, E], F32, name="result")
                nc.scalar.copy(out=result[:], in_=out_bank[g][:])
                nc.sync.dma_start(out=out[batch(g), head(g)].rearrange("(p t) e -> p t e", t=PACK), in_=result[:])

        load_qk(0)
        km_rows = keep.tile([P, H, PACK, E], BF16)
        nc.sync.dma_start(
            out=km_rows[:].rearrange("p h t e -> p h (t e)"), in_=km.rearrange("h (p t) e -> p h (t e)", t=PACK)
        )
        scale_cols = keep.tile([P, PACK], F32)
        nc.sync.dma_start(out=scale_cols[:], in_=v_scale.rearrange("a b (p t) c -> p (a b t c)", t=PACK))
        for g in range(V_BATCH):
            load_v(g)
        load_qk(1)
        gate_rows = []
        for name, gate in (("tg_rows", tg), ("mg_rows", mg)):
            spread = keep.tile([P, H * S], BF16, name=name)
            nc.sync.dma_start(out=spread[:], in_=gate.rearrange("h s -> (h s)").partition_broadcast(P))
            gate_rows.append(spread)
        vm_rows = keep.tile([P, H, PACK, E], BF16)
        nc.sync.dma_start(
            out=vm_rows[:].rearrange("p h t e -> p h (t e)"), in_=vm.rearrange("h (p t) e -> p h (t e)", t=PACK)
        )
        for g in range(V_BATCH, 2 * V_BATCH):
            load_v(g)

        warm = keep.tile([P, 1], F32)
        nc.vector.memset(warm[:], 0.0)
        nc.scalar.activation(out=warm[:], in_=warm[:], func=ACT.Exp)

        ident_bf16 = keep.tile([P, P], BF16)
        make_identity(nc, ident_bf16[:])
        ident_f32 = keep.tile([P, P], F32)
        make_identity(nc, ident_f32[:])

        turn_q(0)
        turn_k(0)
        km_bank = psum.tile([P, H * PACK, P], BF16, name="out_bank")
        for h in range(H):
            turn_rows(km_bank, h, km_rows[:, h])
        km_t = keep.tile([P, H * PACK, P], BF16)
        copy_qk(0)
        nc.vector.tensor_copy(out=km_t[:], in_=km_bank[:])

        for t in range(PACK):
            widen_v(t)

        gates = keep.tile([P, H, 2, KEYS], BF16)
        vm_inter = keep.tile([P, H, E, PACK], BF16, align_bytes=64)
        for h in range(H):
            for half in range(2):
                nc.gpsimd.tensor_scalar(
                    out=gates[:, h, 0, half * S : (half + 1) * S].rearrange("x (u p e) -> x u p e", u=2, e=2),
                    in0=gate_rows[half][:, h * S : (h + 1) * S].rearrange("x (p u e) -> x u p e", u=2, e=2),
                    scalar1=1.0,
                    scalar2=0.0,
                    op0=ALU.mult,
                    op1=ALU.add,
                )
        vm_codes = keep.tile([P, H * E], U32, align_bytes=64)
        vm_scales = keep.tile([P, H * E], U8, align_bytes=64)

        logits(0, 0, 0)
        logits(0, 1, 0)
        logits(0, 0, 1)
        load_qk(2)
        turn_q(1)
        turn_k(1)

        for g in range(GROUPS):
            load_qk(g + 3)
            load_v(g + 2 * V_BATCH)
            quantize_probs(g - 3)
            quantize_v(g - 2)
            if g == 2:
                nc.vector.quantize_mx(
                    out=vm_codes[:].bitcast(FP8X4),
                    scales=vm_scales[:],
                    in_=vm_inter[:].rearrange("p h e t -> p (h e t)"),
                )
            if g == 1:
                nc.vector.tensor_copy(out=gates[:, :, 1, :], in_=gates[:, :, 0, :])
            reciprocals(g - 1, 0)
            weigh_on_pool(g - 1)
            copy_probs(g - 2, 3)
            exponentials(g - 1, 3)
            spread_gates(g - 1)
            turn_probs(g - 2, 0)
            turn_probs(g - 2, 1)
            mix_values(g - 3)
            copy_probs(g - 2, 0)
            copy_probs(g - 2, 1)
            store(g - 3)
            if g == 1:
                vm_bank = psum.tile([P, H, E, PACK], BF16, name="out_bank")
                for h in range(H):
                    interleave(vm_bank[:, h], vm_rows[:, h])
                nc.scalar.copy(out=vm_inter[:], in_=vm_bank[:])

            scan_logits(g, 0, 0)
            logits(g, 2, 0)
            scan_logits(g, 1, 0)
            logits(g, 1, 1)
            scan_logits(g, 0, 1)
            logits(g, 3, 0)
            exponentials(g, 0)
            copy_qk(g + 1)
            if g > 0:
                widen_v(PACK + g - 1)
            reciprocals(g - 1, 1)
            weigh_on_vector(g - 1, 1)
            weigh_on_vector(g - 1, 2)
            turn_probs(g - 1, 2)
            copy_probs(g - 1, 2)
            scan_logits(g, 2, 0)
            logits(g, 2, 1)
            scan_logits(g, 1, 1)
            logits(g, 3, 1)
            exponentials(g, 1)
            scan_logits(g, 3, 0)
            logits(g + 1, 0, 0)
            interleave_v(g - 1)
            turn_q(g + 2)
            weigh_on_vector(g - 1, 3)
            turn_probs(g - 1, 3)
            scan_logits(g, 2, 1)
            logits(g + 1, 1, 0)
            turn_k(g + 2)
            exponentials(g, 2)
            scan_logits(g, 3, 1)
            logits(g + 1, 0, 1)
            copy_v(g - 1)

        last = GROUPS - 1
        quantize_probs(last - 2)
        quantize_v(last - 1)
        reciprocals(last, 0)
        weigh_on_pool(last)
        weigh_on_vector(last, 0)
        weigh_on_vector(last, 1)
        copy_probs(last - 1, 3)
        exponentials(last, 3)
        turn_probs(last - 1, 0)
        turn_probs(last - 1, 1)
        mix_values(last - 2)
        copy_probs(last - 1, 0)
        copy_probs(last - 1, 1)
        store(last - 2)
        interleave_v(last, "rows_bank")
        copy_v(last)
        reciprocals(last, 1)
        weigh_on_vector(last, 2)
        weigh_on_vector(last, 3)
        turn_probs(last, 2)
        turn_probs(last, 1)
        turn_probs(last, 0, "logit_bank0")
        turn_probs(last, 3, "logit_bank1")
        quantize_probs(last - 1)
        copy_probs(last, 2)
        copy_probs(last, 1)
        copy_probs(last, 0)
        copy_probs(last, 3, nc.vector.tensor_copy)
        quantize_v(last)
        mix_values(last - 1)
        quantize_probs(last)
        store(last - 1)
        mix_values(last)
        store(last)
